import numpy as np
import ml_dtypes


def mxq(x, axis, fmt="e4m3"):
    dtype, down = {"e4m3": (ml_dtypes.float8_e4m3fn, 7), "e5m2": (ml_dtypes.float8_e5m2, 14)}[fmt]
    v = np.moveaxis(np.asarray(x, np.float32).astype(ml_dtypes.bfloat16).astype(np.float64), axis, -1)
    blocks = v.reshape(v.shape[:-1] + (-1, 32))
    amax = np.abs(blocks).max(-1, keepdims=True)
    byte = np.maximum(np.where(amax > 0, np.frexp(amax)[1] - 1 + 127, 0) - down, 1)
    scale = np.exp2(byte - 127.0)
    codes = (blocks / scale).astype(np.float32).astype(dtype).astype(np.float64)
    return np.moveaxis((codes * scale).reshape(v.shape), -1, axis)


WIDE = False


def mx_kscale(k):
    if not WIDE:
        return np.ones(k)
    levels = np.array([10, -10, 5, -5, 0])
    if k % 512:
        return np.exp2(np.random.permutation(np.resize(levels, k // 32))).repeat(32)
    a = np.empty((k // 512, 16))
    for p in range(k // 512):
        a[p, :8] = np.random.permutation(np.resize(levels, 8))
        for g in range(8):
            far = levels[np.abs(levels - a[p, g]) >= 10]
            a[p, g + 8] = far[np.random.randint(len(far))]
    return np.exp2(a.ravel()).repeat(32)


def f64(x):
    return np.asarray(x).astype(np.float64)


def striped8(idx):
    return np.concatenate([v.reshape(-1, 16).T for v in idx]).astype(np.uint16)


def unstriped8(offs):
    return np.stack([offs[16 * g:16 * g + 16].T.reshape(-1) for g in range(8)]).astype(np.int64)


E2M1 = np.array([0.0, 0.5, 1.0, 1.5, 2.0, 3.0, 4.0, 6.0, -0.0, -0.5, -1.0, -1.5, -2.0, -3.0, -4.0, -6.0])


def pack_weight(w, fmt):
    k, n = w.shape
    w = f64(np.asarray(w, np.float32).astype(ml_dtypes.bfloat16)).reshape(k // 32, 32, n)
    amax = np.abs(w).max(1)
    if fmt == "e4m3":
        byte = np.frexp(amax)[1] - 1 + 127 - 7
    else:
        mant, ex = np.frexp(amax / 6.0)
        byte = np.where(mant > 0.5, ex, ex - 1) + 127
    byte = np.clip(np.where(amax > 0, byte, 1), 1, 254)
    scaled = (w * np.exp2(127.0 - byte)[:, None, :]).reshape(k, n).astype(np.float32)
    by_word = np.ascontiguousarray(scaled.reshape(k // 512, 128, 4, n).transpose(0, 1, 3, 2))
    if fmt == "e4m3":
        words = by_word.astype(ml_dtypes.float8_e4m3fn).view(np.uint8)
    else:
        c = by_word.astype(ml_dtypes.float4_e2m1fn).view(np.uint8) & 0xF
        words = (c[..., 0::2] | (c[..., 1::2] << 4)).reshape(k // 512, 128, 2 * n)
    return np.ascontiguousarray(words), np.ascontiguousarray(byte.astype(np.uint8).reshape(k // 512, 16, n))


def unpack_weight(words, scales, fmt):
    g, _, n = scales.shape
    words = np.ascontiguousarray(words).reshape(g, 128, n, -1)
    if fmt == "e4m3":
        vals = words.view(ml_dtypes.float8_e4m3fn).astype(np.float64)
    else:
        nib = np.empty((g, 128, n, 4), np.uint8)
        nib[..., 0::2] = words & 0xF
        nib[..., 1::2] = words >> 4
        vals = E2M1[nib]
    vals = vals * np.repeat(np.exp2(scales.astype(np.float64) - 127.0), 8, axis=1)[..., None]
    return vals.transpose(0, 1, 3, 2).reshape(g * 512, n)


def silu(v):
    return v / (1.0 + np.exp(-np.maximum(v, -700.0)))


K, M, T, S = 512, 1024, 2048, 1024


def setup_inputs():
    n = np.random.standard_normal
    s = mx_kscale(K)[:, None]
    p_w4 = pack_weight(n((K, M)) / np.sqrt(K) / s, "e2m1")
    return {
        "xT": (n((K, T)) * s).astype(np.float32),
        "w4_words": p_w4[0],
        "w4_scales": p_w4[1],
        "w8": (n((K, M)) / np.sqrt(K) / s).astype(np.float32),
        "wgt": np.repeat(np.random.uniform(0.5, 2.0, (8, S)), 16, axis=0).astype(np.float32),
        "r": (n((1024, 1024))).astype(np.float32),
        "offs": striped8(np.stack([np.random.permutation(T)[:S] for _ in range(8)])),
    }


def reference(xT, w4_words, w4_scales, w8, wgt, r, offs):
    idx = unstriped8(offs)
    group = np.arange(K) % 512 // 64
    xg = f64(wgt)[np.arange(K) // 4 % 128] * f64(xT)[np.arange(K)[:, None], idx[group]]
    xT_ = mxq(xg, 0, "e4m3")
    w4_ = unpack_weight(w4_words, w4_scales, "e2m1")
    w8_ = mxq(f64(w8), 0, "e4m3")
    y = w4_.T @ xT_
    u = w8_.T @ xT_
    y = silu(y) * u
    return f64(r) + y

from contextlib import ExitStack

import concourse.mybir as mybir
from concourse.masks import make_identity

K, M, T, S = 512, 1024, 2048, 1024
FLOPS = 2 * 2 * K * M * S

F32 = mybir.dt.float32
BF16 = mybir.dt.bfloat16
I32 = mybir.dt.int32
U32 = mybir.dt.uint32
U16 = mybir.dt.uint16
U8 = mybir.dt.uint8
FP8X4 = mybir.dt.float8_e4m3fn_x4
FP4X4 = mybir.dt.float4_e2m1fn_x4
MULT = mybir.AluOpType.mult
ADD = mybir.AluOpType.add
SILU = mybir.ActivationFunctionType.Silu

P = 128
PACK = 4
HALF = 512
BLOCKS = M // P
W8_PIECE = 256

ORDER = [(0, 0), (1, 0), (0, 1), (1, 1)] + [(b, h) for b in range(2, BLOCKS) for h in range(2)]
TURNED = (2, 5, 8, 11, 14)
R_LOADS = ((0, 2), (2, 2), (4, 4))
STORES = {3: (0, 2, 0, S), 7: (2, 2, 0, S), 11: (4, 2, 0, S), 13: (6, 1, 0, S), 14: (7, 1, 0, HALF), 15: (7, 1, HALF, S)}


def interleave(copy, dst, src):
    copy(
        out=dst.rearrange("p (c i) t -> p c t i", i=4),
        in_=src.rearrange("p t (c i) -> p c t i", i=4),
    )


def tile_list_hglu_res_kernel(tc, xT, w4_words, w4_scales, w8, wgt, r, offs, out):
    nc = tc.nc
    with ExitStack() as ctx:
        keep = ctx.enter_context(tc.tile_pool(name="keep", bufs=1))
        ring = ctx.enter_context(tc.tile_pool(name="ring", bufs=4))
        psum = ctx.enter_context(tc.psum_pool(name="psum", bufs=3))
        psum_t = ctx.enter_context(tc.psum_pool(name="psum_t", bufs=2))

        offsets = keep.tile([P, S // 16], U16, name="offsets")
        x_planes = [keep.tile([P, T], F32, name="x%d" % i) for i in range(PACK)]
        weight = [keep.tile([P, HALF], F32, name="wgt%d" % h) for h in range(2)]
        w8_first = keep.tile([P, PACK, W8_PIECE], F32, name="w8first")
        w8_rest = keep.tile([P, PACK, M - W8_PIECE], F32, name="w8rest")
        w4_codes = keep.tile([P, 2 * M], U8, name="w4codes", align_bytes=64)
        w4_plane = keep.tile([P, M], U8, name="w4plane", align_bytes=64)
        r_tiles = [keep.tile([P, n, S], F32, name="r%d" % b0) for b0, n in R_LOADS]
        ident = keep.tile([P, P], F32, name="ident")
        warm = keep.tile([P, 8], F32, name="warm")

        x_rows = xT.rearrange("(p i) t -> p i t", i=PACK)
        w8_rows = w8.rearrange("(p i) n -> p i n", i=PACK)
        r_rows = r.rearrange("(b p) j -> p b j", p=P)
        out_rows = out.rearrange("(b p) j -> p b j", p=P)

        nc.vector.memset(w4_plane[:].bitcast(I32), 0)
        nc.sync.dma_start(offsets[:], offs)
        nc.sync.dma_start(out=x_planes[0][:], in_=x_rows[:, 0, :])
        for q in range(4):
            nc.sync.dma_start(
                out=w4_plane[32 * q : 32 * q + 4, :].bitcast(I32),
                in_=w4_scales[0, 4 * q : 4 * q + 4, :].bitcast(I32),
            )
        nc.sync.dma_start(out=weight[0][:], in_=wgt[:, 0:HALF])
        nc.sync.dma_start(out=weight[1][:], in_=wgt[:, HALF:S])
        nc.sync.dma_start(out=x_planes[1][:], in_=x_rows[:, 1, :])
        nc.sync.dma_start(out=x_planes[2][:], in_=x_rows[:, 2, :])
        nc.sync.dma_start(out=x_planes[3][:], in_=x_rows[:, 3, :])
        nc.sync.dma_start(out=w8_first[:], in_=w8_rows[:, :, 0:W8_PIECE])
        nc.sync.dma_start(out=w4_codes[:].bitcast(I32), in_=w4_words[0].bitcast(I32))
        nc.sync.dma_start(out=w8_rest[:], in_=w8_rows[:, :, W8_PIECE:M])
        for (b0, n), tile in zip(R_LOADS, r_tiles):
            nc.sync.dma_start(out=tile[:], in_=r_rows[:, b0 : b0 + n, :])

        make_identity(nc, ident[:])
        nc.vector.memset(warm[:], 0.0)
        nc.scalar.activation(out=warm[:], in_=warm[:], func=SILU)

        def quantize(name, raw, copy):
            width = raw.shape[2]
            grouped = keep.tile([P, width, PACK], BF16, name=name + "bf", align_bytes=64)
            codes = keep.tile([P, width], U32, name=name + "codes", align_bytes=64)
            plane = keep.tile([P, width], U8, name=name + "plane", align_bytes=64)
            interleave(copy, grouped[:], raw)
            nc.vector.quantize_mx(
                out=codes[:].bitcast(FP8X4),
                scales=plane[:],
                in_=grouped[:].rearrange("p j t -> p (j t)"),
            )
            return codes, plane

        picked = [keep.tile([P, PACK, HALF], F32, name="picked%d" % h) for h in range(2)]

        def gather(i, h):
            nc.vector.tensor_tensor(
                picked[h][:, i, :],
                x_planes[i][:].indirect(offsets[:, 32 * h : 32 * h + 32]),
                weight[h][:],
                MULT,
            )

        w8q = [None] * 4
        xq = [None, None]
        for i in range(PACK):
            gather(i, 0)
            gather(i, 1)
        xq[0] = quantize("xa", picked[0][:], nc.vector.tensor_copy)
        w8q[0] = quantize("w80", w8_first[:], nc.scalar.copy)
        xq[1] = quantize("xb", picked[1][:], nc.scalar.copy)

        def r_slice(b, c0, c1, n=1):
            for (b0, cnt), tile in zip(R_LOADS, r_tiles):
                if b0 <= b < b0 + cnt:
                    return tile[:, b - b0 : b - b0 + n, c0:c1]
            raise ValueError("block")

        for u, (b, h) in enumerate(ORDER):
            if u in (2, 6, 10):
                c = (u + 2) // 4
                w8q[c] = quantize("w8%d" % c, w8_rest[:, :, (c - 1) * W8_PIECE : c * W8_PIECE], nc.scalar.copy)
            x_codes, x_plane = xq[h]
            w8_codes, w8_plane = w8q[b // 2]
            c8 = slice((b % 2) * P, (b % 2 + 1) * P)
            w4c = w4_codes[:, 2 * P * b : 2 * P * (b + 1)].bitcast(FP4X4)
            w4s = w4_plane[:, P * b : P * (b + 1)]
            w8c = w8_codes[:, c8].bitcast(FP8X4)
            w8s = w8_plane[:, c8]
            gate = psum.tile([P, HALF], F32, name="gate")
            up = psum.tile([P, HALF], F32, name="up")
            if u in TURNED:
                for acc, wc, ws in ((gate, w4c, w4s), (up, w8c, w8s)):
                    for a in range(4):
                        cols = slice(a * P, (a + 1) * P)
                        nc.tensor.matmul_mx(
                            out=acc[:, cols],
                            lhsT=x_codes[:, cols].bitcast(FP8X4),
                            lhsT_scale=x_plane[:, cols],
                            rhs=wc,
                            rhs_scale=ws,
                            start=True,
                            stop=True,
                        )
            else:
                for acc, wc, ws in ((gate, w4c, w4s), (up, w8c, w8s)):
                    nc.tensor.matmul_mx(
                        out=acc[:],
                        lhsT=wc,
                        lhsT_scale=ws,
                        rhs=x_codes[:].bitcast(FP8X4),
                        rhs_scale=x_plane[:],
                        start=True,
                        stop=True,
                    )
            act = ring.tile([P, HALF], F32, name="act")
            nc.scalar.activation(out=act[:], in_=gate[:], func=SILU)
            y = ring.tile([P, HALF], F32, name="y")
            nc.vector.tensor_tensor(y[:], up[:], act[:], MULT)
            res = r_slice(b, h * HALF, (h + 1) * HALF)[:, 0, :]
            if u in TURNED:
                back = psum_t.tile([P, HALF], F32, name="back")
                for a in range(4):
                    cols = slice(a * P, (a + 1) * P)
                    nc.tensor.transpose(back[:, cols], y[:, cols], ident[:])
                nc.vector.tensor_tensor(res, back[:], res, ADD)
            elif u == len(ORDER) - 1:
                nc.vector.tensor_tensor(res, y[:], res, ADD)
            else:
                nc.gpsimd.tensor_tensor(res, y[:], res, ADD)
            if u in STORES:
                b0, n, c0, c1 = STORES[u]
                nc.sync.dma_start(out=out_rows[:, b0 : b0 + n, c0:c1], in_=r_slice(b0, c0, c1, n))
